import numpy as np, ml_dtypes
CORES = [32,40,48,56,64,72,80,88,96,104,112,120]
N = 12
F = 128
def setup_inputs(rng):
    m = (rng.standard_normal((N, 128, 128), dtype=np.float32) / 11).astype(ml_dtypes.bfloat16)
    return {"m": m, "mt": m.transpose(0, 2, 1).copy(), "x": rng.standard_normal((N, 128, F), dtype=np.float32).astype(ml_dtypes.bfloat16)}
def setup_inputs_big(rng):
    d = setup_inputs(rng)
    for k in ("x",): d[k] = (d[k].astype(np.float32) * 1048576.0).astype(d[k].dtype)
    return d
def setup_inputs_small(rng):
    d = setup_inputs(rng)
    for k in ("x",): d[k] = (d[k].astype(np.float32) * (1 / 1048576.0)).astype(d[k].dtype)
    return d
def setup_inputs_apart(rng):
    d = setup_inputs(rng)
    f = (10.0 ** rng.permutation(np.linspace(-1.5, 1.5, N))).astype(np.float32).reshape(N, 1, 1)
    for k in ("x",): d[k] = (d[k].astype(np.float32) * f).astype(d[k].dtype)
    return d
def reference(m, mt, x):
    M, X = m.astype(np.float64), x.astype(np.float64)
    y = np.zeros((N, 128, F)); p = X[0]
    for r in range(N):
        p = M[r].T @ p
        y[r] = p
    return {"y": y.astype(ml_dtypes.bfloat16)}

@@ -1,0 +1,253 @@
+from concourse.bass import DstId, RemoteDMATransfer
+
+N = 12
+D = 128
+WINDOW = 12
+NREL = 4
+BOTH_DIES = True
+E_DRAM = 8
+E_SBUF = 16
+NOPS = 12
+NBANK = 8
+
+SCRATCH = {
+    "om": ("sbuf", [128, D], "bfloat16"),
+    "xs": ("sbuf", [128, D], "bfloat16"),
+    "land": ("sbuf", [128, N * D], "bfloat16"),
+    "prod": ("sbuf", [128, NOPS * D], "bfloat16"),
+    "fw": ("dram", [128, D], "bfloat16"),
+    "rl": ("dram", [128, D], "bfloat16"),
+}
+for _b in range(NBANK):
+    SCRATCH["ps%d" % _b] = ("psum", [128, 512], "float32")
+SEMAPHORES = (["ldm", "ldt", "ldx", "st", "snd", "rin"] + ["a%d" % k for k in range(N)]
+              + ["mm%d" % i for i in range(NOPS)] + ["cp%d" % i for i in range(NOPS)])
+
+
+def _base(r):
+    return max(0, r - WINDOW)
+
+
+def _tree(r):
+    tab, nodes, order = [], [], []
+    for k in range(_base(r) + 1, r + 1):
+        tab.append(["leaf", k, None, None])
+        nodes.append(len(tab) - 1)
+    while len(nodes) > 1:
+        new, i = [], len(nodes)
+        while i >= 2:
+            tab.append(["node", nodes[i - 2], nodes[i - 1], None])
+            new.append(len(tab) - 1)
+            order.append(len(tab) - 1)
+            i -= 2
+        if i == 1:
+            new.append(nodes[0])
+        new.reverse()
+        nodes = new
+    root = nodes[0]
+    tab[root][3] = "T"
+    for i in order:
+        tab[tab[i][1]][3] = "S"
+        tab[tab[i][2]][3] = "T"
+    return tab, order, root
+
+
+def _form(k, r):
+    for e in _tree(r)[0]:
+        if e[0] == "leaf" and e[1] == k:
+            return e[3]
+    return None
+
+
+def _prio(r):
+    feeds = any(_base(q) == r for q in range(r + 1, N)) and r > 0
+    return (1 if feeds else 0, r)
+
+
+def _bits(mask):
+    return [b for b in range(mask.bit_length()) if (mask >> b) & 1]
+
+
+def _take(mask, n):
+    out = 0
+    for b in _bits(mask)[:n]:
+        out |= 1 << b
+    return out
+
+
+def _sends(k, cores, topo):
+    me = cores[k]
+    items = [(r, _form(k, r)) for r in range(k + 1, N) if _base(r) < k]
+    items += [(r, "P") for r in range(k + 1, N) if _base(r) == k]
+    items.sort(key=lambda it: _prio(it[0]), reverse=True)
+    direct = {"S": [], "T": [], "P": []}
+    far = []
+    for r, f in items:
+        if topo.may_write(me, cores[r]):
+            direct[f].append(r)
+        else:
+            far.append((r, f))
+    lanes, what = [], None
+    if far:
+        kinds = sorted(set(f for _, f in far))
+        assert len(kinds) == 1 and kinds[0] in ("S", "P")
+        what = kinds[0]
+        chipmates = [c for c in range(topo.CHIPS * topo.CORES_PER_CHIP)
+                     if topo.chip(c) == topo.chip(me) and c != me]
+        owners = [c for c in chipmates if all(topo.may_write(c, cores[r]) for r, _ in far)]
+        near = [c for c in owners if topo.die(c) == topo.die(me)]
+        away = [c for c in owners if topo.die(c) != topo.die(me)]
+        pool = []
+        if BOTH_DIES:
+            for i in range(max(len(near), len(away))):
+                pool += near[i:i + 1] + away[i:i + 1]
+        else:
+            pool = near + away
+        pool = pool[:NREL]
+        rot = k // 2 if BOTH_DIES else 0
+        for i, (r, _) in enumerate(far):
+            c = pool[(i + rot) % len(pool)]
+            for ln in lanes:
+                if ln[0] == c:
+                    ln[1].append(r)
+                    break
+            else:
+                lanes.append((c, [r]))
+    return direct, lanes, what
+
+
+def _write(g, T, topo, src_core, dst_cores, out_ap, in_ap, sem, mask):
+    n = len(_bits(mask))
+    if len(dst_cores) == 1:
+        rid, pid, _ = topo.addr(dst_cores[0])
+        g.remote_dma(out_ap=out_ap, in_ap=in_ap, remote_sem=sem, local_sem=T.sem.snd, pid=pid, routing_id=rid,
+                     dma_engine_mask=mask)
+        return n
+    ids = []
+    for c in dst_cores:
+        rid, pid, _ = topo.addr(c)
+        ids.append(DstId(rid=rid, pnc=pid))
+    g.remote_dma_fused([RemoteDMATransfer(dst_ids=ids, dma_engine_mask=mask, remote_sem=sem, srcs=[in_ap],
+                                          dsts=[out_ap for _ in dst_cores], alu_op=0)], local_sem=T.sem.snd)
+    return n
+
+
+def _relay_program(g, core, T, topo):
+    cores = T.cores
+    for k in range(N):
+        if topo.chip(cores[k]) != topo.chip(core):
+            continue
+        _, lanes, what = _sends(k, cores, topo)
+        for c, ranks in lanes:
+            if c != core:
+                continue
+            n_in = E_SBUF if what == "P" else E_DRAM
+            g.wait_ge(T.sem.rin, n_in)
+            sent = 0
+            for r in ranks:
+                sent += _write(g, T, topo, core, [cores[r]], T.land[:, k * D:(k + 1) * D], T.rl[:],
+                               T.sem["a%d" % k], topo.mask(core, cores[r]))
+            g.wait_ge(T.sem.snd, sent)
+
+
+def rank_program(g, core, T, topo):
+    rank = T.rank_of(core)
+    if rank is None:
+        _relay_program(g, core, T, topo)
+        return
+    cores = T.cores
+    direct, lanes, what = _sends(rank, cores, topo)
+    slot = T.land[:, rank * D:(rank + 1) * D]
+    arr = T.sem["a%d" % rank]
+
+    need_mt = bool(direct["S"]) or what == "S"
+    if need_mt:
+        g.sync.dma_start(T.fw[:], T.mt[:]).then_inc(T.sem.ldt, 16)
+    g.scalar.dma_start(T.om[:], T.m[:]).then_inc(T.sem.ldm, 16)
+    if rank == 0:
+        g.sync.dma_start(T.xs[:], T.x[:]).then_inc(T.sem.ldx, 16)
+
+    tab, order, root = _tree(rank) if rank > 0 else ([], [], None)
+    opno = {}
+    seen = set()
+
+    def wait_t(name, val):
+        if name not in seen:
+            seen.add(name)
+            g.tensor.wait_ge(T.sem[name], val)
+
+    def operand(i):
+        e = tab[i]
+        if e[0] == "node":
+            j = opno[i]
+            wait_t("cp%d" % j, 1)
+            return T.prod[:, j * D:(j + 1) * D]
+        k = e[1]
+        if k == rank:
+            assert e[3] == "T"
+            wait_t("ldm", 16)
+            return T.om[:]
+        return landed(k)
+
+    def landed(k):
+        wait_t("a%d" % k, len(_bits(topo.mask(cores[k], core))))
+        return T.land[:, k * D:(k + 1) * D]
+
+    def product(j, lhsT, rhs):
+        if j >= NBANK:
+            wait_t("cp%d" % (j - NBANK), 1)
+        ps = T["ps%d" % (j % NBANK)][:, 0:D]
+        g.tensor.matmul(ps, lhsT, rhs, start=True, stop=True).then_inc(T.sem["mm%d" % j], 1)
+        g.vector.wait_ge(T.sem["mm%d" % j], 1)
+        g.vector.tensor_copy(T.prod[:, j * D:(j + 1) * D], ps).then_inc(T.sem["cp%d" % j], 1)
+
+    j = 0
+    for i in order:
+        left, right = operand(tab[i][1]), operand(tab[i][2])
+        if tab[i][3] == "T":
+            product(j, left, right)
+        else:
+            product(j, right, left)
+        opno[i] = j
+        j += 1
+    if rank == 0:
+        wait_t("ldm", 16)
+        wait_t("ldx", 16)
+        product(j, T.om[:], T.xs[:])
+    else:
+        v = operand(root)
+        product(j, v, landed(_base(rank)))
+    last = j
+    res = T.prod[:, last * D:(last + 1) * D]
+
+    g.sync.wait_ge(T.sem["cp%d" % last], 1)
+    g.sync.dma_start(T.y[:], res).then_inc(T.sem.st, 16)
+    g.sync.wait_ge(T.sem.st, 16)
+
+    sent = 0
+
+    def to_relays(src, n_eng):
+        rc = [c for c, _ in lanes]
+        return _write(g, T, topo, core, rc, T.rl[:], src, T.sem.rin, _take(topo.mask(core, rc[0]), n_eng))
+
+    def to_ranks(ranks, src):
+        dc = [cores[r] for r in ranks]
+        return _write(g, T, topo, core, dc, slot, src, arr, topo.mask(core, dc[0]))
+
+    if need_mt:
+        g.wait_ge(T.sem.ldt, 16)
+        if what == "S":
+            sent += to_relays(T.fw[:], E_DRAM)
+        if direct["S"]:
+            sent += to_ranks(direct["S"], T.fw[:])
+    if direct["T"]:
+        g.wait_ge(T.sem.ldm, 16)
+        sent += to_ranks(direct["T"], T.om[:])
+    if what == "P" or direct["P"]:
+        g.wait_ge(T.sem["cp%d" % last], 1)
+        if what == "P":
+            sent += to_relays(res, E_SBUF)
+        if direct["P"]:
+            sent += to_ranks(direct["P"], res)
+    if sent:
+        g.wait_ge(T.sem.snd, sent)

@@ -2,13 +2,12 @@ from concourse.bass import DstId, RemoteDMATransfer
 
 N = 12
 D = 128
-WINDOW = 12
 NREL = 4
-BOTH_DIES = True
-E_DRAM = 8
-E_SBUF = 16
+E_ON = 8
 NOPS = 12
 NBANK = 8
+T_MM, T_CP = 0.09, 0.13
+AT_OWN, AT_DIRECT, AT_RELAYED, AT_P0, AT_SECOND = -3.0, -1.0, 0.0, 1.0, 0.5
 
 SCRATCH = {
     "om": ("sbuf", [128, D], "bfloat16"),
@@ -16,52 +15,52 @@ SCRATCH = {
     "land": ("sbuf", [128, N * D], "bfloat16"),
     "prod": ("sbuf", [128, NOPS * D], "bfloat16"),
     "fw": ("dram", [128, D], "bfloat16"),
+    "fm": ("dram", [128, D], "bfloat16"),
     "rl": ("dram", [128, D], "bfloat16"),
 }
 for _b in range(NBANK):
     SCRATCH["ps%d" % _b] = ("psum", [128, 512], "float32")
-SEMAPHORES = (["ldm", "ldt", "ldx", "st", "snd", "rin"] + ["a%d" % k for k in range(N)]
+SEMAPHORES = (["ldm", "ldt", "ldf", "ldx", "st", "snd", "rin"] + ["a%d" % k for k in range(N)]
               + ["mm%d" % i for i in range(NOPS)] + ["cp%d" % i for i in range(NOPS)])
 
 
-def _base(r):
-    return max(0, r - WINDOW)
+def _tree(r, cores, topo):
+    def direct(k, q):
+        return topo.may_write(cores[k], cores[q])
 
-
-def _tree(r):
-    tab, nodes, order = [], [], []
-    for k in range(_base(r) + 1, r + 1):
-        tab.append(["leaf", k, None, None])
-        nodes.append(len(tab) - 1)
+    tab = []
+    for k in range(r + 1):
+        if k == r:
+            at = AT_OWN
+        elif direct(k, r):
+            at = AT_DIRECT
+        else:
+            ahead = len([q for q in range(r + 1, N) if not direct(k, q)])
+            at = (AT_P0 if k == 0 else AT_RELAYED) + AT_SECOND * (ahead // NREL)
+        tab.append(["leaf", k, None, None, at])
+    nodes = list(range(r + 1))
+    order = []
+    pe = dv = AT_OWN
     while len(nodes) > 1:
-        new, i = [], len(nodes)
-        while i >= 2:
-            tab.append(["node", nodes[i - 2], nodes[i - 1], None])
-            new.append(len(tab) - 1)
-            order.append(len(tab) - 1)
-            i -= 2
-        if i == 1:
-            new.append(nodes[0])
-        new.reverse()
-        nodes = new
-    root = nodes[0]
-    tab[root][3] = "T"
+        best = None
+        for i in range(len(nodes) - 1):
+            a, b = tab[nodes[i]], tab[nodes[i + 1]]
+            if b[0] == "leaf" and b[1] != r and not direct(b[1], r):
+                continue
+            t = max(a[4], b[4])
+            if best is None or t <= best[0]:
+                best = (t, i)
+        t, i = best
+        pe = max(t, pe) + T_MM
+        dv = max(pe, dv) + T_CP
+        tab.append(["node", nodes[i], nodes[i + 1], None, dv])
+        order.append(len(tab) - 1)
+        nodes[i:i + 2] = [len(tab) - 1]
+    tab[nodes[0]][3] = "S"
     for i in order:
         tab[tab[i][1]][3] = "S"
         tab[tab[i][2]][3] = "T"
-    return tab, order, root
-
-
-def _form(k, r):
-    for e in _tree(r)[0]:
-        if e[0] == "leaf" and e[1] == k:
-            return e[3]
-    return None
-
-
-def _prio(r):
-    feeds = any(_base(q) == r for q in range(r + 1, N)) and r > 0
-    return (1 if feeds else 0, r)
+    return tab, order
 
 
 def _bits(mask):
@@ -77,46 +76,48 @@ def _take(mask, n):
 
 def _sends(k, cores, topo):
     me = cores[k]
-    items = [(r, _form(k, r)) for r in range(k + 1, N) if _base(r) < k]
-    items += [(r, "P") for r in range(k + 1, N) if _base(r) == k]
-    items.sort(key=lambda it: _prio(it[0]), reverse=True)
-    direct = {"S": [], "T": [], "P": []}
+    direct = {"S": [], "T": []}
     far = []
-    for r, f in items:
+    for r in range(N - 1, k, -1):
         if topo.may_write(me, cores[r]):
-            direct[f].append(r)
+            direct[_tree(r, cores, topo)[0][k][3]].append(r)
         else:
-            far.append((r, f))
-    lanes, what = [], None
+            far.append(r)
+    lanes = []
     if far:
-        kinds = sorted(set(f for _, f in far))
-        assert len(kinds) == 1 and kinds[0] in ("S", "P")
-        what = kinds[0]
         chipmates = [c for c in range(topo.CHIPS * topo.CORES_PER_CHIP)
                      if topo.chip(c) == topo.chip(me) and c != me]
-        owners = [c for c in chipmates if all(topo.may_write(c, cores[r]) for r, _ in far)]
+        owners = [c for c in chipmates if all(topo.may_write(c, cores[r]) for r in far)]
         near = [c for c in owners if topo.die(c) == topo.die(me)]
         away = [c for c in owners if topo.die(c) != topo.die(me)]
         pool = []
-        if BOTH_DIES:
-            for i in range(max(len(near), len(away))):
-                pool += near[i:i + 1] + away[i:i + 1]
-        else:
-            pool = near + away
+        for i in range(max(len(near), len(away))):
+            pool += near[i:i + 1] + away[i:i + 1]
         pool = pool[:NREL]
-        rot = k // 2 if BOTH_DIES else 0
-        for i, (r, _) in enumerate(far):
-            c = pool[(i + rot) % len(pool)]
+        for i, r in enumerate(far):
+            c = pool[(i + k // 2) % len(pool)]
             for ln in lanes:
                 if ln[0] == c:
                     ln[1].append(r)
                     break
             else:
                 lanes.append((c, [r]))
-    return direct, lanes, what
+    return direct, lanes
 
 
-def _write(g, T, topo, src_core, dst_cores, out_ap, in_ap, sem, mask):
+def _relay_mask(k, cores, topo, relay):
+    me = cores[k]
+    mask = topo.mask(me, relay)
+    if k == 0:
+        return mask
+    stay = mask
+    for c in cores:
+        if c != me:
+            stay &= ~topo.mask(me, c)
+    return _take(stay if stay else mask, E_ON)
+
+
+def _write(g, T, topo, dst_cores, out_ap, in_ap, sem, mask):
     n = len(_bits(mask))
     if len(dst_cores) == 1:
         rid, pid, _ = topo.addr(dst_cores[0])
@@ -137,15 +138,13 @@ def _relay_program(g, core, T, topo):
     for k in range(N):
         if topo.chip(cores[k]) != topo.chip(core):
             continue
-        _, lanes, what = _sends(k, cores, topo)
-        for c, ranks in lanes:
+        for c, ranks in _sends(k, cores, topo)[1]:
             if c != core:
                 continue
-            n_in = E_SBUF if what == "P" else E_DRAM
-            g.wait_ge(T.sem.rin, n_in)
+            g.wait_ge(T.sem.rin, len(_bits(_relay_mask(k, cores, topo, core))))
             sent = 0
             for r in ranks:
-                sent += _write(g, T, topo, core, [cores[r]], T.land[:, k * D:(k + 1) * D], T.rl[:],
+                sent += _write(g, T, topo, [cores[r]], T.land[:, k * D:(k + 1) * D], T.rl[:],
                                T.sem["a%d" % k], topo.mask(core, cores[r]))
             g.wait_ge(T.sem.snd, sent)
 
@@ -156,27 +155,29 @@ def rank_program(g, core, T, topo):
         _relay_program(g, core, T, topo)
         return
     cores = T.cores
-    direct, lanes, what = _sends(rank, cores, topo)
+    direct, lanes = _sends(rank, cores, topo)
     slot = T.land[:, rank * D:(rank + 1) * D]
     arr = T.sem["a%d" % rank]
 
-    need_mt = bool(direct["S"]) or what == "S"
-    if need_mt:
+    need_fw = rank > 0 and bool(direct["S"] or lanes)
+    need_fm = rank > 0 and bool(direct["T"])
+    if need_fw:
         g.sync.dma_start(T.fw[:], T.mt[:]).then_inc(T.sem.ldt, 16)
+    if need_fm:
+        g.scalar.dma_start(T.fm[:], T.m[:]).then_inc(T.sem.ldf, 16)
     g.scalar.dma_start(T.om[:], T.m[:]).then_inc(T.sem.ldm, 16)
     if rank == 0:
         g.sync.dma_start(T.xs[:], T.x[:]).then_inc(T.sem.ldx, 16)
 
-    tab, order, root = _tree(rank) if rank > 0 else ([], [], None)
-    opno = {}
     seen = set()
+    opno = {}
 
     def wait_t(name, val):
         if name not in seen:
             seen.add(name)
             g.tensor.wait_ge(T.sem[name], val)
 
-    def operand(i):
+    def operand(tab, i):
         e = tab[i]
         if e[0] == "node":
             j = opno[i]
@@ -184,12 +185,8 @@ def rank_program(g, core, T, topo):
             return T.prod[:, j * D:(j + 1) * D]
         k = e[1]
         if k == rank:
-            assert e[3] == "T"
             wait_t("ldm", 16)
             return T.om[:]
-        return landed(k)
-
-    def landed(k):
         wait_t("a%d" % k, len(_bits(topo.mask(cores[k], core))))
         return T.land[:, k * D:(k + 1) * D]
 
@@ -201,23 +198,21 @@ def rank_program(g, core, T, topo):
         g.vector.wait_ge(T.sem["mm%d" % j], 1)
         g.vector.tensor_copy(T.prod[:, j * D:(j + 1) * D], ps).then_inc(T.sem["cp%d" % j], 1)
 
-    j = 0
-    for i in order:
-        left, right = operand(tab[i][1]), operand(tab[i][2])
-        if tab[i][3] == "T":
-            product(j, left, right)
-        else:
-            product(j, right, left)
-        opno[i] = j
-        j += 1
     if rank == 0:
         wait_t("ldm", 16)
         wait_t("ldx", 16)
-        product(j, T.om[:], T.xs[:])
+        product(0, T.om[:], T.xs[:])
+        last = 0
     else:
-        v = operand(root)
-        product(j, v, landed(_base(rank)))
-    last = j
+        tab, order = _tree(rank, cores, topo)
+        for j, i in enumerate(order):
+            left, right = operand(tab, tab[i][1]), operand(tab, tab[i][2])
+            if tab[i][3] == "T":
+                product(j, left, right)
+            else:
+                product(j, right, left)
+            opno[i] = j
+        last = len(order) - 1
     res = T.prod[:, last * D:(last + 1) * D]
 
     g.sync.wait_ge(T.sem["cp%d" % last], 1)
@@ -225,29 +220,17 @@ def rank_program(g, core, T, topo):
     g.sync.wait_ge(T.sem.st, 16)
 
     sent = 0
-
-    def to_relays(src, n_eng):
-        rc = [c for c, _ in lanes]
-        return _write(g, T, topo, core, rc, T.rl[:], src, T.sem.rin, _take(topo.mask(core, rc[0]), n_eng))
-
-    def to_ranks(ranks, src):
-        dc = [cores[r] for r in ranks]
-        return _write(g, T, topo, core, dc, slot, src, arr, topo.mask(core, dc[0]))
-
-    if need_mt:
-        g.wait_ge(T.sem.ldt, 16)
-        if what == "S":
-            sent += to_relays(T.fw[:], E_DRAM)
-        if direct["S"]:
-            sent += to_ranks(direct["S"], T.fw[:])
-    if direct["T"]:
-        g.wait_ge(T.sem.ldm, 16)
-        sent += to_ranks(direct["T"], T.om[:])
-    if what == "P" or direct["P"]:
-        g.wait_ge(T.sem["cp%d" % last], 1)
-        if what == "P":
-            sent += to_relays(res, E_SBUF)
-        if direct["P"]:
-            sent += to_ranks(direct["P"], res)
+    src = {"S": T.fw[:], "T": T.fm[:]} if rank > 0 else {"S": res, "T": res}
+    gate = {"S": ("ldt", 16), "T": ("ldf", 16)} if rank > 0 else {"S": ("cp0", 1), "T": ("cp0", 1)}
+    plan = (["relays"] if lanes else []) + [f for f in ("T", "S") if direct[f]]
+    for what in plan:
+        name, val = gate["S" if what == "relays" else what]
+        g.wait_ge(T.sem[name], val)
+        if what == "relays":
+            rc = [c for c, _ in lanes]
+            sent += _write(g, T, topo, rc, T.rl[:], src["S"], T.sem.rin, _relay_mask(rank, cores, topo, rc[0]))
+        else:
+            dc = [cores[r] for r in direct[what]]
+            sent += _write(g, T, topo, dc, slot, src[what], arr, topo.mask(core, dc[0]))
     if sent:
         g.wait_ge(T.sem.snd, sent)

from concourse.bass import DstId, RemoteDMATransfer

N = 12
D = 128
NREL = 4
E_ON = 8
NOPS = 12
NBANK = 8
T_MM, T_CP = 0.09, 0.13
AT_OWN, AT_DIRECT, AT_RELAYED, AT_P0, AT_SECOND = -3.0, -1.0, 0.0, 1.0, 0.5

SCRATCH = {
    "om": ("sbuf", [128, D], "bfloat16"),
    "xs": ("sbuf", [128, D], "bfloat16"),
    "land": ("sbuf", [128, N * D], "bfloat16"),
    "prod": ("sbuf", [128, NOPS * D], "bfloat16"),
    "fw": ("dram", [128, D], "bfloat16"),
    "fm": ("dram", [128, D], "bfloat16"),
    "rl": ("dram", [128, D], "bfloat16"),
}
for _b in range(NBANK):
    SCRATCH["ps%d" % _b] = ("psum", [128, 512], "float32")
SEMAPHORES = (["ldm", "ldt", "ldf", "ldx", "st", "snd", "rin"] + ["a%d" % k for k in range(N)]
              + ["mm%d" % i for i in range(NOPS)] + ["cp%d" % i for i in range(NOPS)])


def _tree(r, cores, topo):
    def direct(k, q):
        return topo.may_write(cores[k], cores[q])

    tab = []
    for k in range(r + 1):
        if k == r:
            at = AT_OWN
        elif direct(k, r):
            at = AT_DIRECT
        else:
            ahead = len([q for q in range(r + 1, N) if not direct(k, q)])
            at = (AT_P0 if k == 0 else AT_RELAYED) + AT_SECOND * (ahead // NREL)
        tab.append(["leaf", k, None, None, at])
    nodes = list(range(r + 1))
    order = []
    pe = dv = AT_OWN
    while len(nodes) > 1:
        best = None
        for i in range(len(nodes) - 1):
            a, b = tab[nodes[i]], tab[nodes[i + 1]]
            if b[0] == "leaf" and b[1] != r and not direct(b[1], r):
                continue
            t = max(a[4], b[4])
            if best is None or t <= best[0]:
                best = (t, i)
        t, i = best
        pe = max(t, pe) + T_MM
        dv = max(pe, dv) + T_CP
        tab.append(["node", nodes[i], nodes[i + 1], None, dv])
        order.append(len(tab) - 1)
        nodes[i:i + 2] = [len(tab) - 1]
    tab[nodes[0]][3] = "S"
    for i in order:
        tab[tab[i][1]][3] = "S"
        tab[tab[i][2]][3] = "T"
    return tab, order


def _bits(mask):
    return [b for b in range(mask.bit_length()) if (mask >> b) & 1]


def _take(mask, n):
    out = 0
    for b in _bits(mask)[:n]:
        out |= 1 << b
    return out


def _sends(k, cores, topo):
    me = cores[k]
    direct = {"S": [], "T": []}
    far = []
    for r in range(N - 1, k, -1):
        if topo.may_write(me, cores[r]):
            direct[_tree(r, cores, topo)[0][k][3]].append(r)
        else:
            far.append(r)
    lanes = []
    if far:
        chipmates = [c for c in range(topo.CHIPS * topo.CORES_PER_CHIP)
                     if topo.chip(c) == topo.chip(me) and c != me]
        owners = [c for c in chipmates if all(topo.may_write(c, cores[r]) for r in far)]
        near = [c for c in owners if topo.die(c) == topo.die(me)]
        away = [c for c in owners if topo.die(c) != topo.die(me)]
        pool = []
        for i in range(max(len(near), len(away))):
            pool += near[i:i + 1] + away[i:i + 1]
        pool = pool[:NREL]
        for i, r in enumerate(far):
            c = pool[(i + k // 2) % len(pool)]
            for ln in lanes:
                if ln[0] == c:
                    ln[1].append(r)
                    break
            else:
                lanes.append((c, [r]))
    return direct, lanes


def _relay_mask(k, cores, topo, relay):
    me = cores[k]
    mask = topo.mask(me, relay)
    if k == 0:
        return mask
    stay = mask
    for c in cores:
        if c != me:
            stay &= ~topo.mask(me, c)
    return _take(stay if stay else mask, E_ON)


def _write(g, T, topo, dst_cores, out_ap, in_ap, sem, mask):
    n = len(_bits(mask))
    if len(dst_cores) == 1:
        rid, pid, _ = topo.addr(dst_cores[0])
        g.remote_dma(out_ap=out_ap, in_ap=in_ap, remote_sem=sem, local_sem=T.sem.snd, pid=pid, routing_id=rid,
                     dma_engine_mask=mask)
        return n
    ids = []
    for c in dst_cores:
        rid, pid, _ = topo.addr(c)
        ids.append(DstId(rid=rid, pnc=pid))
    g.remote_dma_fused([RemoteDMATransfer(dst_ids=ids, dma_engine_mask=mask, remote_sem=sem, srcs=[in_ap],
                                          dsts=[out_ap for _ in dst_cores], alu_op=0)], local_sem=T.sem.snd)
    return n


def _relay_program(g, core, T, topo):
    cores = T.cores
    for k in range(N):
        if topo.chip(cores[k]) != topo.chip(core):
            continue
        for c, ranks in _sends(k, cores, topo)[1]:
            if c != core:
                continue
            g.wait_ge(T.sem.rin, len(_bits(_relay_mask(k, cores, topo, core))))
            sent = 0
            for r in ranks:
                sent += _write(g, T, topo, [cores[r]], T.land[:, k * D:(k + 1) * D], T.rl[:],
                               T.sem["a%d" % k], topo.mask(core, cores[r]))
            g.wait_ge(T.sem.snd, sent)


def rank_program(g, core, T, topo):
    rank = T.rank_of(core)
    if rank is None:
        _relay_program(g, core, T, topo)
        return
    cores = T.cores
    direct, lanes = _sends(rank, cores, topo)
    slot = T.land[:, rank * D:(rank + 1) * D]
    arr = T.sem["a%d" % rank]

    need_fw = rank > 0 and bool(direct["S"] or lanes)
    need_fm = rank > 0 and bool(direct["T"])
    if need_fw:
        g.sync.dma_start(T.fw[:], T.mt[:]).then_inc(T.sem.ldt, 16)
    if need_fm:
        g.scalar.dma_start(T.fm[:], T.m[:]).then_inc(T.sem.ldf, 16)
    g.scalar.dma_start(T.om[:], T.m[:]).then_inc(T.sem.ldm, 16)
    if rank == 0:
        g.sync.dma_start(T.xs[:], T.x[:]).then_inc(T.sem.ldx, 16)

    seen = set()
    opno = {}

    def wait_t(name, val):
        if name not in seen:
            seen.add(name)
            g.tensor.wait_ge(T.sem[name], val)

    def operand(tab, i):
        e = tab[i]
        if e[0] == "node":
            j = opno[i]
            wait_t("cp%d" % j, 1)
            return T.prod[:, j * D:(j + 1) * D]
        k = e[1]
        if k == rank:
            wait_t("ldm", 16)
            return T.om[:]
        wait_t("a%d" % k, len(_bits(topo.mask(cores[k], core))))
        return T.land[:, k * D:(k + 1) * D]

    def product(j, lhsT, rhs):
        if j >= NBANK:
            wait_t("cp%d" % (j - NBANK), 1)
        ps = T["ps%d" % (j % NBANK)][:, 0:D]
        g.tensor.matmul(ps, lhsT, rhs, start=True, stop=True).then_inc(T.sem["mm%d" % j], 1)
        g.vector.wait_ge(T.sem["mm%d" % j], 1)
        g.vector.tensor_copy(T.prod[:, j * D:(j + 1) * D], ps).then_inc(T.sem["cp%d" % j], 1)

    if rank == 0:
        wait_t("ldm", 16)
        wait_t("ldx", 16)
        product(0, T.om[:], T.xs[:])
        last = 0
    else:
        tab, order = _tree(rank, cores, topo)
        for j, i in enumerate(order):
            left, right = operand(tab, tab[i][1]), operand(tab, tab[i][2])
            if tab[i][3] == "T":
                product(j, left, right)
            else:
                product(j, right, left)
            opno[i] = j
        last = len(order) - 1
    res = T.prod[:, last * D:(last + 1) * D]

    g.sync.wait_ge(T.sem["cp%d" % last], 1)
    g.sync.dma_start(T.y[:], res).then_inc(T.sem.st, 16)
    g.sync.wait_ge(T.sem.st, 16)

    sent = 0
    src = {"S": T.fw[:], "T": T.fm[:]} if rank > 0 else {"S": res, "T": res}
    gate = {"S": ("ldt", 16), "T": ("ldf", 16)} if rank > 0 else {"S": ("cp0", 1), "T": ("cp0", 1)}
    plan = (["relays"] if lanes else []) + [f for f in ("T", "S") if direct[f]]
    for what in plan:
        name, val = gate["S" if what == "relays" else what]
        g.wait_ge(T.sem[name], val)
        if what == "relays":
            rc = [c for c, _ in lanes]
            sent += _write(g, T, topo, rc, T.rl[:], src["S"], T.sem.rin, _relay_mask(rank, cores, topo, rc[0]))
        else:
            dc = [cores[r] for r in direct[what]]
            sent += _write(g, T, topo, dc, slot, src[what], arr, topo.mask(core, dc[0]))
    if sent:
        g.wait_ge(T.sem.snd, sent)
